import numpy as np
import ml_dtypes


def mxq(x, axis, fmt="e4m3"):
    dtype, down = {"e4m3": (ml_dtypes.float8_e4m3fn, 7), "e5m2": (ml_dtypes.float8_e5m2, 14)}[fmt]
    v = np.moveaxis(np.asarray(x, np.float32).astype(ml_dtypes.bfloat16).astype(np.float64), axis, -1)
    blocks = v.reshape(v.shape[:-1] + (-1, 32))
    amax = np.abs(blocks).max(-1, keepdims=True)
    byte = np.maximum(np.where(amax > 0, np.frexp(amax)[1] - 1 + 127, 0) - down, 1)
    scale = np.exp2(byte - 127.0)
    codes = (blocks / scale).astype(np.float32).astype(dtype).astype(np.float64)
    return np.moveaxis((codes * scale).reshape(v.shape), -1, axis)


WIDE = False


def mx_kscale(k):
    if not WIDE:
        return np.ones(k)
    levels = np.array([10, -10, 5, -5, 0])
    if k % 512:
        return np.exp2(np.random.permutation(np.resize(levels, k // 32))).repeat(32)
    a = np.empty((k // 512, 16))
    for p in range(k // 512):
        a[p, :8] = np.random.permutation(np.resize(levels, 8))
        for g in range(8):
            far = levels[np.abs(levels - a[p, g]) >= 10]
            a[p, g + 8] = far[np.random.randint(len(far))]
    return np.exp2(a.ravel()).repeat(32)


BF16 = ml_dtypes.bfloat16


def bf(x):
    return np.asarray(x, np.float32).astype(BF16)


def f64(x):
    return np.asarray(x).astype(np.float64)


E2M1 = np.array([0.0, 0.5, 1.0, 1.5, 2.0, 3.0, 4.0, 6.0, -0.0, -0.5, -1.0, -1.5, -2.0, -3.0, -4.0, -6.0])


def pack_weight(w, fmt):
    k, n = w.shape
    w = f64(bf(w)).reshape(k // 32, 32, n)
    amax = np.abs(w).max(1)
    if fmt == "e4m3":
        byte = np.frexp(amax)[1] - 1 + 127 - 7
    else:
        mant, ex = np.frexp(amax / 6.0)
        byte = np.where(mant > 0.5, ex, ex - 1) + 127
    byte = np.clip(np.where(amax > 0, byte, 1), 1, 254)
    scaled = (w * np.exp2(127.0 - byte)[:, None, :]).reshape(k, n).astype(np.float32)
    by_word = np.ascontiguousarray(scaled.reshape(k // 512, 128, 4, n).transpose(0, 1, 3, 2))
    if fmt == "e4m3":
        words = by_word.astype(ml_dtypes.float8_e4m3fn).view(np.uint8)
    else:
        c = by_word.astype(ml_dtypes.float4_e2m1fn).view(np.uint8) & 0xF
        words = c[..., 0::2] | (c[..., 1::2] << 4)
    return np.ascontiguousarray(words), np.ascontiguousarray(byte.astype(np.uint8).reshape(k // 512, 16, n))


def unpack_weight(words, scales, fmt):
    g, p, n, _ = words.shape
    if fmt == "e4m3":
        vals = np.ascontiguousarray(words).view(ml_dtypes.float8_e4m3fn).astype(np.float64)
    else:
        nib = np.empty((g, p, n, 4), np.uint8)
        nib[..., 0::2] = words & 0xF
        nib[..., 1::2] = words >> 4
        vals = E2M1[nib]
    vals = vals * np.repeat(np.exp2(scales.astype(np.float64) - 127.0), 8, axis=1)[..., None]
    return vals.transpose(0, 1, 3, 2).reshape(g * 512, n)
def pack4(w):
    words, scales = pack_weight(w, "e2m1")
    return words.reshape(words.shape[0], 128, -1), scales


def unpack4(words, scales):
    return unpack_weight(words.reshape(words.shape[0], 128, -1, 2), scales, "e2m1")


M, F, D, T = 2048, 1024, 1024, 512

KAPPA = 0.2


def setup_inputs():
    s = mx_kscale(M)
    r = mx_kscale(D)
    v = mx_kscale(F)
    size = F ** -0.25
    l = np.random.standard_normal((D, F)) * size / np.sqrt(D) * r[:, None]
    e = np.random.standard_normal((D, F)) / r[:, None] * v
    l_words, l_scales = pack4(l)
    e_words, e_scales = pack4(e)
    a = np.random.standard_normal((M, F)) * s[:, None] / v
    b = np.random.standard_normal((M, T)) * size / np.sqrt(M) / s[:, None]
    d = 0.5 * np.random.standard_normal((F, T)) * size / v[:, None]
    c = 0.5 * np.random.standard_normal((F, T)) - KAPPA
    return {"l_words": l_words, "l_scales": l_scales,
            "e_words": e_words, "e_scales": e_scales,
            "a": bf(a), "b": bf(b), "d": bf(d), "c": bf(c)}


def reference(l_words, l_scales, e_words, e_scales, a, b, d, c):
    l = unpack4(l_words, l_scales)
    e = unpack4(e_words, e_scales)
    h = l.T @ e
    y = mxq(f64(a), 0, "e4m3").T @ mxq(f64(b), 0, "e4m3")
    rhs = y + f64(d)
    x = mxq(h, 1, "e4m3") @ mxq(rhs, 0, "e4m3")
    return np.maximum(x + f64(c), 0.0)

@@ -1,0 +1,277 @@
+from contextlib import ExitStack
+
+import concourse.mybir as mybir
+
+M, F, D, T = 2048, 1024, 1024, 512
+FLOPS = 2 * D * F * F + 2 * M * F * T + 2 * F * F * T
+
+F32 = mybir.dt.float32
+BF16 = mybir.dt.bfloat16
+I32 = mybir.dt.int32
+U32 = mybir.dt.uint32
+U8 = mybir.dt.uint8
+FP8X4 = mybir.dt.float8_e4m3fn_x4
+FP4X4 = mybir.dt.float4_e2m1fn_x4
+ADD = mybir.AluOpType.add
+RELU = mybir.ActivationFunctionType.Relu
+
+P = 128
+PACK = 4
+KP = P * PACK
+RUNS = 32
+SAMPLE_PASSES = M // KP
+GROUPS = F // KP
+FACTOR_PASSES = D // KP
+HALF = T // 2
+SHARE_FIRST, SHARE_H, SHARE_LATE = 10, 8, 20
+
+
+def tile_admm_nonnegative_lasso_step_s12_kernel(
+    tc, l_words, l_scales, e_words, e_scales, a, b, d, c, out
+):
+    nc = tc.nc
+    with ExitStack() as ctx:
+        keep = ctx.enter_context(tc.tile_pool(name="keep", bufs=1))
+        stage = ctx.enter_context(tc.tile_pool(name="stage", bufs=3))
+        psum = ctx.enter_context(tc.psum_pool(name="psum", bufs=1))
+        ctx.enter_context(tc.manual_schedule())
+
+        def held(name, shape, dtype):
+            tile = keep.tile(shape, dtype, name=name, tag=name, align_bytes=64)
+            return tile
+
+        def bank(number, shape):
+            tile = psum.tile(shape, F32, name="bank%d" % number, tag="bank%d" % number)
+            return tile
+
+        chunks = [("b", 0, k) for k in range(SAMPLE_PASSES)]
+        chunks.extend(("a", g, k) for g in range(GROUPS) for k in range(SAMPLE_PASSES))
+        raw = [held("raw%d" % n, [P, PACK, KP], BF16) for n in range(len(chunks))]
+        codes = [held("codes%d" % n, [P, KP], U32) for n in range(len(chunks))]
+        scales = [held("scales%d" % n, [P, KP], U8) for n in range(len(chunks))]
+        l_half = [held("l_half%d" % g, [P, FACTOR_PASSES, 2 * KP], U8) for g in range(GROUPS)]
+        e_raw = [held("e_raw%d" % g, [P, FACTOR_PASSES, 2 * KP], U8) for g in range(GROUPS)]
+        e_half = [held("e_half%d" % g, [P, FACTOR_PASSES, 2 * KP], U8) for g in range(GROUPS)]
+        l_plane = held("l_plane", [P, FACTOR_PASSES, F], U8)
+        e_plane_raw = held("e_plane_raw", [P, FACTOR_PASSES, F], U8)
+        e_plane = held("e_plane", [P, FACTOR_PASSES, F], U8)
+        d_sb = [held("d_sb%d" % g, [P, PACK, T], BF16) for g in range(GROUPS)]
+        c_sb = [held("c_sb%d" % h, [P, F // P, HALF], BF16) for h in range(2)]
+        h_codes = [held("h_codes%d" % g, [P, F], U32) for g in range(GROUPS)]
+        h_scales = [held("h_scales%d" % g, [P, F], U8) for g in range(GROUPS)]
+        r_codes = [held("r_codes%d" % g, [P, T], U32) for g in range(GROUPS)]
+        r_scales = [held("r_scales%d" % g, [P, T], U8) for g in range(GROUPS)]
+        r_sum = [held("r_sum%d" % g, [P, PACK, T], BF16) for g in range(GROUPS)]
+        r_grouped = [held("r_grouped%d" % g, [P, T * PACK], BF16) for g in range(GROUPS)]
+        warm = held("warm", [P, 16], F32)
+
+        def load_chunk(n):
+            which, g, k = chunks[n]
+            rows = slice(k * KP, (k + 1) * KP)
+            src = b[rows, :] if which == "b" else a[rows, g * KP : (g + 1) * KP]
+            nc.sync.dma_start(out=raw[n][:], in_=src.rearrange("(p j) w -> p j w", j=PACK))
+
+        def load_words(tile, words, g):
+            src = words[:, :, 2 * KP * g : 2 * KP * (g + 1)].rearrange("k p n -> p k n")
+            nc.sync.dma_start(out=tile[:].bitcast(I32), in_=src.bitcast(I32))
+
+        def load_plane(queue, plane, rows):
+            by_r = rows.rearrange("k (q r) n -> r q k n", r=4)
+            for r in range(4):
+                queue.dma_start(out=plane[r:P:32, :, :].bitcast(I32), in_=by_r[r].bitcast(I32))
+
+        def load_d(g):
+            by_i = d[g * KP : (g + 1) * KP, :].rearrange("(u t i) n -> i u t n", t=PACK, i=4)
+            for i in range(4):
+                nc.sync.dma_start(out=d_sb[g][i:P:4, :, :], in_=by_i[i])
+
+        nc.vector.memset(e_plane_raw[:].bitcast(I32), 0)
+        nc.vector.memset(l_plane[:].bitcast(I32), 0)
+        nc.vector.memset(warm[:, 0:8], 0.0)
+        nc.scalar.activation(out=warm[:, 8:16], in_=warm[:, 0:8], func=RELU)
+
+        load_chunk(0)
+        load_words(e_raw[0], e_words, 0)
+        load_plane(nc.sync, e_plane_raw, e_scales)
+        load_words(l_half[0], l_words, 0)
+        load_chunk(1)
+        load_plane(nc.sync, l_plane, l_scales)
+        load_chunk(2)
+        load_words(e_raw[1], e_words, 1)
+        load_words(l_half[1], l_words, 1)
+        for n in range(3, 9):
+            load_chunk(n)
+        load_d(0)
+        for n in range(9, 12):
+            load_chunk(n)
+        load_d(1)
+        c_rows = c.rearrange("(j p) n -> p j n", p=P)
+        out_rows = out.rearrange("(j p) n -> p j n", p=P)
+        for h in range(2):
+            nc.sync.dma_start(out=c_sb[h][:], in_=c_rows[:, :, h * HALF : (h + 1) * HALF])
+
+        def order_e_plane():
+            nc.vector.tensor_copy(
+                out=e_plane[:].bitcast(I32).rearrange("p k (g t u) -> p k g t u", g=GROUPS, t=PACK),
+                in_=e_plane_raw[:].bitcast(I32).rearrange("p k (g u t) -> p k g t u", g=GROUPS, t=PACK),
+            )
+
+        def order_e_words(g):
+            nc.vector.tensor_copy(
+                out=e_half[g][:].bitcast(I32).rearrange("p k (t u w) -> p k t u w", t=PACK, w=2),
+                in_=e_raw[g][:].bitcast(I32).rearrange("p k (u t w) -> p k t u w", t=PACK, w=2),
+            )
+
+        def interleave(dst, src, permute, lo, hi, engine):
+            s = src.rearrange("p j (u t i) -> p u t j i", t=PACK, i=4)
+            if permute:
+                o = dst.rearrange("p (t u i j) -> p u t j i", t=PACK, i=4, j=PACK)
+            else:
+                o = dst.rearrange("p (u t i j) -> p u t j i", t=PACK, i=4, j=PACK)
+            if engine == "vector":
+                nc.vector.tensor_copy(out=o[:, lo:hi], in_=s[:, lo:hi])
+            else:
+                nc.scalar.copy(out=o[:, lo:hi], in_=s[:, lo:hi])
+
+        def quantize(codes_ap, scales_ap, src):
+            nc.vector.quantize_mx(out=codes_ap.bitcast(FP8X4), scales=scales_ap, in_=src)
+
+        h_units = [(g, 4 * hf + jj) for hf in range(2) for g in range(GROUPS) for jj in range(4)]
+        h_banks = {}
+        h_grouped = {}
+
+        def h_matmul(n):
+            g, j = h_units[n]
+            acc = bank(4 + n % 4, [P, PACK, P])
+            h_banks[n] = acc
+            hf, jj = divmod(j, 4)
+            for t in range(PACK):
+                for k in range(FACTOR_PASSES):
+                    nc.tensor.matmul_mx(
+                        out=acc[:, t, :],
+                        lhsT=e_half[g][:, k, 2 * P * t : 2 * P * (t + 1)].bitcast(FP4X4),
+                        lhsT_scale=e_plane[:, k, g * KP + P * t : g * KP + P * (t + 1)],
+                        rhs=l_half[hf][:, k, 2 * P * jj : 2 * P * (jj + 1)].bitcast(FP4X4),
+                        rhs_scale=l_plane[:, k, P * j : P * (j + 1)],
+                        start=(k == 0),
+                        stop=(k == FACTOR_PASSES - 1),
+                    )
+
+        def h_copy(n):
+            q, jj = divmod(n, 4)
+            if jj == 0:
+                h_grouped[q] = stage.tile([P, KP * PACK], BF16, name="h_grouped", tag="h_grouped", bufs=2, align_bytes=64)
+            dst = h_grouped[q][:, KP * jj : KP * (jj + 1)].rearrange("p (n t) -> p n t", t=PACK)
+            nc.scalar.copy(out=dst, in_=h_banks[n][:].rearrange("p t n -> p n t"))
+
+        def h_quantize(q):
+            g, j = h_units[4 * q]
+            cols = slice(P * j, P * j + KP)
+            quantize(h_codes[g][:, cols], h_scales[g][:, cols], h_grouped[q][:])
+
+        r_banks = {}
+
+        def rhs_pass(n):
+            which, g, k = chunks[n]
+            if k == 0:
+                r_banks[g] = [bank(t, [P, T]) for t in range(PACK)]
+            for t in range(PACK):
+                cols = slice(P * t, P * (t + 1))
+                nc.tensor.matmul_mx(
+                    out=r_banks[g][t][:],
+                    lhsT=codes[n][:, cols].bitcast(FP8X4),
+                    lhsT_scale=scales[n][:, cols],
+                    rhs=codes[k][:].bitcast(FP8X4),
+                    rhs_scale=scales[k][:],
+                    start=(k == 0),
+                    stop=(k == SAMPLE_PASSES - 1),
+                )
+
+        def rhs_add(g, cols):
+            for t in range(PACK):
+                nc.vector.tensor_tensor(
+                    out=r_sum[g][:, t, cols], in0=r_banks[g][t][:, cols], in1=d_sb[g][:, t, cols], op=ADD
+                )
+
+        def rhs_interleave(g, lo, hi):
+            interleave(r_grouped[g][:], r_sum[g][:], False, lo, hi, "scalar")
+
+        def rhs_quantize(g, cols):
+            quantize(r_codes[g][:, cols], r_scales[g][:, cols], r_grouped[g][:, PACK * cols.start : PACK * cols.stop])
+
+        grouped = {}
+        last = len(chunks) - 1
+        for n in range(len(chunks)):
+            which = chunks[n][0]
+            share = SHARE_FIRST if n == 0 else SHARE_H if n <= 8 else SHARE_LATE
+            if n >= 2 and chunks[n - 2][0] == "a":
+                rhs_pass(n - 2)
+            if 1 <= n <= 8:
+                h_matmul(2 * n - 2)
+                h_matmul(2 * n - 1)
+            if 2 <= n <= 9:
+                h_copy(2 * n - 4)
+                h_copy(2 * n - 3)
+            grouped[n] = stage.tile([P, KP * PACK], BF16, name="grouped", tag="grouped", bufs=3, align_bytes=64)
+            interleave(grouped[n][:], raw[n][:], which == "a", RUNS - share, RUNS, "scalar")
+            if n == 10:
+                rhs_interleave(0, 0, RUNS)
+            interleave(grouped[n][:], raw[n][:], which == "a", 0, RUNS - share, "vector")
+            if n >= 1:
+                quantize(codes[n - 1][:], scales[n - 1][:], grouped[n - 1][:])
+            if n == 0:
+                order_e_plane()
+                order_e_words(0)
+            if n == 2:
+                order_e_words(1)
+            if n in (4, 6, 8, 10):
+                h_quantize((n - 4) // 2)
+            if n == 9:
+                rhs_add(0, slice(0, T))
+        rhs_pass(last - 1)
+        quantize(codes[last][:], scales[last][:], grouped[last][:])
+        rhs_pass(last)
+        rhs_quantize(0, slice(0, T))
+
+        halves = [slice(h * HALF, (h + 1) * HALF) for h in range(2)]
+        for h in range(2):
+            rhs_add(1, halves[h])
+            rhs_interleave(1, h * RUNS // 2, (h + 1) * RUNS // 2)
+
+        x_banks = {}
+
+        def x_matmul(h, pair):
+            acc = bank(4 * (1 - h) + pair, [P, 2, HALF])
+            x_banks[h, pair] = acc
+            for jj in range(2):
+                cols = slice(P * (2 * pair + jj), P * (2 * pair + jj + 1))
+                for g in range(GROUPS):
+                    nc.tensor.matmul_mx(
+                        out=acc[:, jj, :],
+                        lhsT=h_codes[g][:, cols].bitcast(FP8X4),
+                        lhsT_scale=h_scales[g][:, cols],
+                        rhs=r_codes[g][:, halves[h]].bitcast(FP8X4),
+                        rhs_scale=r_scales[g][:, halves[h]],
+                        start=(g == 0),
+                        stop=(g == GROUPS - 1),
+                    )
+
+        def x_finish(h, pair):
+            rows = slice(2 * pair, 2 * pair + 2)
+            total = stage.tile([P, 2, HALF], F32, name="total", tag="total", bufs=4)
+            nc.vector.tensor_tensor(out=total[:], in0=x_banks[h, pair][:], in1=c_sb[h][:, rows, :], op=ADD)
+            result = stage.tile([P, 2, HALF], F32, name="result", tag="result", bufs=8)
+            nc.scalar.activation(out=result[:], in_=total[:], func=RELU)
+            nc.sync.dma_start(out=out_rows[:, rows, halves[h]], in_=result[:])
+
+        rhs_quantize(1, halves[0])
+        for pair in range(4):
+            x_matmul(0, pair)
+        x_finish(0, 0)
+        rhs_quantize(1, halves[1])
+        for pair in range(4):
+            x_matmul(1, pair)
+        for pair in range(1, 4):
+            x_finish(0, pair)
+        for pair in range(4):
+            x_finish(1, pair)

@@ -13,17 +13,24 @@ U8 = mybir.dt.uint8
 FP8X4 = mybir.dt.float8_e4m3fn_x4
 FP4X4 = mybir.dt.float4_e2m1fn_x4
 ADD = mybir.AluOpType.add
-RELU = mybir.ActivationFunctionType.Relu
+ACT = mybir.ActivationFunctionType
 
 P = 128
-PACK = 4
-KP = P * PACK
-RUNS = 32
-SAMPLE_PASSES = M // KP
-GROUPS = F // KP
-FACTOR_PASSES = D // KP
+SLOTS = 4
+PASS = P * SLOTS
+RUN = 4
+STRIPS = PASS // (RUN * SLOTS)
+SAMPLE_PASSES = M // PASS
+FACTOR_PASSES = D // PASS
+GROUPS = F // PASS
 HALF = T // 2
-SHARE_FIRST, SHARE_H, SHARE_LATE = 10, 8, 20
+QUARTER = T // 4
+
+SHARE_BESIDE_H, SHARE_EVEN, SHARE_BESIDE_ADDS = 12, 16, 24
+H_EARLY = 12
+H_PER_STEP = 2
+H_LEAD = 2
+LOAD_BOUND_STEPS = 3
 
 
 def tile_admm_nonnegative_lasso_step_s12_kernel(
@@ -32,7 +39,7 @@ def tile_admm_nonnegative_lasso_step_s12_kernel(
     nc = tc.nc
     with ExitStack() as ctx:
         keep = ctx.enter_context(tc.tile_pool(name="keep", bufs=1))
-        stage = ctx.enter_context(tc.tile_pool(name="stage", bufs=3))
+        stage = ctx.enter_context(tc.tile_pool(name="stage", bufs=4))
         psum = ctx.enter_context(tc.psum_pool(name="psum", bufs=1))
         ctx.enter_context(tc.manual_schedule())
 
@@ -44,234 +51,270 @@ def tile_admm_nonnegative_lasso_step_s12_kernel(
             tile = psum.tile(shape, F32, name="bank%d" % number, tag="bank%d" % number)
             return tile
 
-        chunks = [("b", 0, k) for k in range(SAMPLE_PASSES)]
-        chunks.extend(("a", g, k) for g in range(GROUPS) for k in range(SAMPLE_PASSES))
-        raw = [held("raw%d" % n, [P, PACK, KP], BF16) for n in range(len(chunks))]
-        codes = [held("codes%d" % n, [P, KP], U32) for n in range(len(chunks))]
-        scales = [held("scales%d" % n, [P, KP], U8) for n in range(len(chunks))]
-        l_half = [held("l_half%d" % g, [P, FACTOR_PASSES, 2 * KP], U8) for g in range(GROUPS)]
-        e_raw = [held("e_raw%d" % g, [P, FACTOR_PASSES, 2 * KP], U8) for g in range(GROUPS)]
-        e_half = [held("e_half%d" % g, [P, FACTOR_PASSES, 2 * KP], U8) for g in range(GROUPS)]
-        l_plane = held("l_plane", [P, FACTOR_PASSES, F], U8)
-        e_plane_raw = held("e_plane_raw", [P, FACTOR_PASSES, F], U8)
-        e_plane = held("e_plane", [P, FACTOR_PASSES, F], U8)
-        d_sb = [held("d_sb%d" % g, [P, PACK, T], BF16) for g in range(GROUPS)]
-        c_sb = [held("c_sb%d" % h, [P, F // P, HALF], BF16) for h in range(2)]
+        chunks = [(b, 0, k) for k in range(SAMPLE_PASSES)]
+        chunks.extend((a, g, k) for g in range(GROUPS) for k in range(SAMPLE_PASSES))
+        first_a = SAMPLE_PASSES
+        last = len(chunks) - 1
+        raw = [held("raw%d" % n, [P, SLOTS, PASS], BF16) for n in range(len(chunks))]
+        codes = [held("codes%d" % n, [P, PASS], U32) for n in range(len(chunks))]
+        scales = [held("scales%d" % n, [P, PASS], U8) for n in range(len(chunks))]
+        l_codes = [held("l_codes%d" % q, [P, FACTOR_PASSES, 2 * PASS], U8) for q in range(GROUPS)]
+        e_loaded = [held("e_loaded%d" % g, [P, FACTOR_PASSES, 2 * PASS], U8) for g in range(GROUPS)]
+        e_codes = [held("e_codes%d" % g, [P, FACTOR_PASSES, 2 * PASS], U8) for g in range(GROUPS)]
+        l_scale_tile = held("l_scale_tile", [P, FACTOR_PASSES, F], U8)
+        e_scale_loaded = held("e_scale_loaded", [P, FACTOR_PASSES, F], U8)
+        e_scale_tile = held("e_scale_tile", [P, FACTOR_PASSES, F], U8)
+        d_sb = [held("d_sb%d" % g, [P, SLOTS, T], BF16) for g in range(GROUPS)]
+        c_sb = [held("c_sb%d" % q, [P, SLOTS, T], BF16) for q in range(GROUPS)]
         h_codes = [held("h_codes%d" % g, [P, F], U32) for g in range(GROUPS)]
         h_scales = [held("h_scales%d" % g, [P, F], U8) for g in range(GROUPS)]
-        r_codes = [held("r_codes%d" % g, [P, T], U32) for g in range(GROUPS)]
-        r_scales = [held("r_scales%d" % g, [P, T], U8) for g in range(GROUPS)]
-        r_sum = [held("r_sum%d" % g, [P, PACK, T], BF16) for g in range(GROUPS)]
-        r_grouped = [held("r_grouped%d" % g, [P, T * PACK], BF16) for g in range(GROUPS)]
-        warm = held("warm", [P, 16], F32)
+        rhs_sum = [held("rhs_sum%d" % g, [P, SLOTS, T], BF16) for g in range(GROUPS)]
+        rhs_grouped = [held("rhs_grouped%d" % g, [P, T * SLOTS], BF16) for g in range(GROUPS)]
+        rhs_codes = [held("rhs_codes%d" % g, [P, T], U32) for g in range(GROUPS)]
+        rhs_scales = [held("rhs_scales%d" % g, [P, T], U8) for g in range(GROUPS)]
+        c_rows = c.rearrange("(q p j) n -> p q j n", p=P, j=SLOTS)
+        out_rows = out.rearrange("(q p j) n -> p q j n", p=P, j=SLOTS)
+
 
         def load_chunk(n):
-            which, g, k = chunks[n]
-            rows = slice(k * KP, (k + 1) * KP)
-            src = b[rows, :] if which == "b" else a[rows, g * KP : (g + 1) * KP]
-            nc.sync.dma_start(out=raw[n][:], in_=src.rearrange("(p j) w -> p j w", j=PACK))
+            source, g, k = chunks[n]
+            rows = source[k * PASS : (k + 1) * PASS, g * PASS : (g + 1) * PASS]
+            nc.sync.dma_start(out=raw[n][:], in_=rows.rearrange("(p s) w -> p s w", s=SLOTS))
 
-        def load_words(tile, words, g):
-            src = words[:, :, 2 * KP * g : 2 * KP * (g + 1)].rearrange("k p n -> p k n")
-            nc.sync.dma_start(out=tile[:].bitcast(I32), in_=src.bitcast(I32))
+        def load_codes(tile, words, g):
+            columns = words[:, :, 2 * PASS * g : 2 * PASS * (g + 1)].rearrange("k p n -> p k n")
+            nc.sync.dma_start(out=tile[:].bitcast(I32), in_=columns.bitcast(I32))
 
-        def load_plane(queue, plane, rows):
+        def load_scales(tile, rows):
             by_r = rows.rearrange("k (q r) n -> r q k n", r=4)
             for r in range(4):
-                queue.dma_start(out=plane[r:P:32, :, :].bitcast(I32), in_=by_r[r].bitcast(I32))
+                nc.sync.dma_start(out=tile[r:P:32, :, :].bitcast(I32), in_=by_r[r].bitcast(I32))
 
         def load_d(g):
-            by_i = d[g * KP : (g + 1) * KP, :].rearrange("(u t i) n -> i u t n", t=PACK, i=4)
-            for i in range(4):
-                nc.sync.dma_start(out=d_sb[g][i:P:4, :, :], in_=by_i[i])
+            by_i = d[g * PASS : (g + 1) * PASS, :].rearrange("(u s i) n -> i u s n", s=SLOTS, i=RUN)
+            for i in range(RUN):
+                nc.sync.dma_start(out=d_sb[g][i:P:RUN, :, :], in_=by_i[i])
 
-        nc.vector.memset(e_plane_raw[:].bitcast(I32), 0)
-        nc.vector.memset(l_plane[:].bitcast(I32), 0)
-        nc.vector.memset(warm[:, 0:8], 0.0)
-        nc.scalar.activation(out=warm[:, 8:16], in_=warm[:, 0:8], func=RELU)
+        nc.vector.memset(e_scale_loaded[:].bitcast(I32), 0)
+        nc.vector.memset(l_scale_tile[:].bitcast(I32), 0)
 
         load_chunk(0)
-        load_words(e_raw[0], e_words, 0)
-        load_plane(nc.sync, e_plane_raw, e_scales)
-        load_words(l_half[0], l_words, 0)
+        load_codes(e_loaded[0], e_words, 0)
+        load_scales(e_scale_loaded, e_scales)
+        load_codes(l_codes[0], l_words, 0)
+        load_scales(l_scale_tile, l_scales)
         load_chunk(1)
-        load_plane(nc.sync, l_plane, l_scales)
+        load_codes(e_loaded[1], e_words, 1)
         load_chunk(2)
-        load_words(e_raw[1], e_words, 1)
-        load_words(l_half[1], l_words, 1)
-        for n in range(3, 9):
+        load_codes(l_codes[1], l_words, 1)
+        for n in range(3, last - 1):
             load_chunk(n)
         load_d(0)
-        for n in range(9, 12):
-            load_chunk(n)
+        load_chunk(last - 1)
+        load_chunk(last)
         load_d(1)
-        c_rows = c.rearrange("(j p) n -> p j n", p=P)
-        out_rows = out.rearrange("(j p) n -> p j n", p=P)
-        for h in range(2):
-            nc.sync.dma_start(out=c_sb[h][:], in_=c_rows[:, :, h * HALF : (h + 1) * HALF])
+        for q in range(GROUPS):
+            nc.sync.dma_start(out=c_sb[q][:], in_=c_rows[:, q, :, :])
 
-        def order_e_plane():
+
+        def order_e_scales():
             nc.vector.tensor_copy(
-                out=e_plane[:].bitcast(I32).rearrange("p k (g t u) -> p k g t u", g=GROUPS, t=PACK),
-                in_=e_plane_raw[:].bitcast(I32).rearrange("p k (g u t) -> p k g t u", g=GROUPS, t=PACK),
+                out=e_scale_tile[:].bitcast(I32).rearrange("p k (g s u) -> p k g s u", g=GROUPS, s=SLOTS),
+                in_=e_scale_loaded[:].bitcast(I32).rearrange("p k (g u s) -> p k g s u", g=GROUPS, s=SLOTS),
             )
 
-        def order_e_words(g):
+        def order_e_codes(g):
             nc.vector.tensor_copy(
-                out=e_half[g][:].bitcast(I32).rearrange("p k (t u w) -> p k t u w", t=PACK, w=2),
-                in_=e_raw[g][:].bitcast(I32).rearrange("p k (u t w) -> p k t u w", t=PACK, w=2),
+                out=e_codes[g][:].bitcast(I32).rearrange("p k (s u w) -> p k s u w", s=SLOTS, w=2),
+                in_=e_loaded[g][:].bitcast(I32).rearrange("p k (u s w) -> p k s u w", s=SLOTS, w=2),
             )
 
-        def interleave(dst, src, permute, lo, hi, engine):
-            s = src.rearrange("p j (u t i) -> p u t j i", t=PACK, i=4)
-            if permute:
-                o = dst.rearrange("p (t u i j) -> p u t j i", t=PACK, i=4, j=PACK)
-            else:
-                o = dst.rearrange("p (u t i j) -> p u t j i", t=PACK, i=4, j=PACK)
-            if engine == "vector":
-                nc.vector.tensor_copy(out=o[:, lo:hi], in_=s[:, lo:hi])
-            else:
-                nc.scalar.copy(out=o[:, lo:hi], in_=s[:, lo:hi])
+        def interleave(copy, grouped, rows, strips, stationary):
+            order = "p (t u i s) -> p u t i s" if stationary else "p (u t i s) -> p u t i s"
+            copy(
+                out=grouped.rearrange(order, t=SLOTS, i=RUN, s=SLOTS)[:, strips],
+                in_=rows.rearrange("p s (u t i) -> p u t i s", t=SLOTS, i=RUN)[:, strips],
+            )
 
-        def quantize(codes_ap, scales_ap, src):
-            nc.vector.quantize_mx(out=codes_ap.bitcast(FP8X4), scales=scales_ap, in_=src)
+        def copy_by_activation(out, in_):
+            nc.scalar.activation(out=out, in_=in_, func=ACT.Copy)
 
-        h_units = [(g, 4 * hf + jj) for hf in range(2) for g in range(GROUPS) for jj in range(4)]
+        def quantize(code_ap, scale_ap, grouped):
+            nc.vector.quantize_mx(out=code_ap.bitcast(FP8X4), scales=scale_ap, in_=grouped)
+
+        chunk_grouped = {}
+
+        def quantize_chunk(n):
+            quantize(codes[n][:], scales[n][:], chunk_grouped[n][:])
+
+        h_sets = [(g, q) for q in range(GROUPS) for g in range(GROUPS)]
         h_banks = {}
         h_grouped = {}
 
-        def h_matmul(n):
-            g, j = h_units[n]
-            acc = bank(4 + n % 4, [P, PACK, P])
-            h_banks[n] = acc
-            hf, jj = divmod(j, 4)
-            for t in range(PACK):
+        def h_matmul(unit):
+            g, q = h_sets[unit // 4]
+            moving = unit % 4
+            acc = bank((4 + unit) % 8 if unit < H_EARLY else 2 + unit % 2, [P, SLOTS, P])
+            h_banks[unit] = acc
+            for s in range(SLOTS):
                 for k in range(FACTOR_PASSES):
                     nc.tensor.matmul_mx(
-                        out=acc[:, t, :],
-                        lhsT=e_half[g][:, k, 2 * P * t : 2 * P * (t + 1)].bitcast(FP4X4),
-                        lhsT_scale=e_plane[:, k, g * KP + P * t : g * KP + P * (t + 1)],
-                        rhs=l_half[hf][:, k, 2 * P * jj : 2 * P * (jj + 1)].bitcast(FP4X4),
-                        rhs_scale=l_plane[:, k, P * j : P * (j + 1)],
+                        out=acc[:, s, :],
+                        lhsT=e_codes[g][:, k, 2 * P * s : 2 * P * (s + 1)].bitcast(FP4X4),
+                        lhsT_scale=e_scale_tile[:, k, g * PASS + P * s : g * PASS + P * (s + 1)],
+                        rhs=l_codes[q][:, k, 2 * P * moving : 2 * P * (moving + 1)].bitcast(FP4X4),
+                        rhs_scale=l_scale_tile[:, k, q * PASS + P * moving : q * PASS + P * (moving + 1)],
                         start=(k == 0),
                         stop=(k == FACTOR_PASSES - 1),
                     )
 
-        def h_copy(n):
-            q, jj = divmod(n, 4)
-            if jj == 0:
-                h_grouped[q] = stage.tile([P, KP * PACK], BF16, name="h_grouped", tag="h_grouped", bufs=2, align_bytes=64)
-            dst = h_grouped[q][:, KP * jj : KP * (jj + 1)].rearrange("p (n t) -> p n t", t=PACK)
-            nc.scalar.copy(out=dst, in_=h_banks[n][:].rearrange("p t n -> p n t"))
+        def h_copy(unit):
+            n, w = divmod(unit, 4)
+            if w == 0:
+                h_grouped[n] = stage.tile([P, PASS * SLOTS], BF16, name="h_grouped", tag="h_grouped", align_bytes=64)
+            target = h_grouped[n][:].rearrange("p (j w m s) -> p w j m s", j=SLOTS, w=4, s=SLOTS)[:, w]
+            nc.scalar.copy(out=target, in_=h_banks[unit][:].rearrange("p s (m j) -> p j m s", j=SLOTS))
 
-        def h_quantize(q):
-            g, j = h_units[4 * q]
-            cols = slice(P * j, P * j + KP)
-            quantize(h_codes[g][:, cols], h_scales[g][:, cols], h_grouped[q][:])
+        def h_quantize(n):
+            g, q = h_sets[n]
+            columns = slice(q * PASS, (q + 1) * PASS)
+            quantize(h_codes[g][:, columns], h_scales[g][:, columns], h_grouped[n][:])
 
-        r_banks = {}
+        rhs_banks = {}
 
         def rhs_pass(n):
-            which, g, k = chunks[n]
+            source, g, k = chunks[n]
             if k == 0:
-                r_banks[g] = [bank(t, [P, T]) for t in range(PACK)]
-            for t in range(PACK):
-                cols = slice(P * t, P * (t + 1))
+                rhs_banks[g] = [bank(SLOTS * g + s, [P, T]) for s in range(SLOTS)]
+            for s in range(SLOTS):
+                columns = slice(P * s, P * (s + 1))
                 nc.tensor.matmul_mx(
-                    out=r_banks[g][t][:],
-                    lhsT=codes[n][:, cols].bitcast(FP8X4),
-                    lhsT_scale=scales[n][:, cols],
+                    out=rhs_banks[g][s][:],
+                    lhsT=codes[n][:, columns].bitcast(FP8X4),
+                    lhsT_scale=scales[n][:, columns],
                     rhs=codes[k][:].bitcast(FP8X4),
                     rhs_scale=scales[k][:],
                     start=(k == 0),
                     stop=(k == SAMPLE_PASSES - 1),
                 )
 
-        def rhs_add(g, cols):
-            for t in range(PACK):
+        def rhs_add(g, lo, hi):
+            for s in range(SLOTS):
                 nc.vector.tensor_tensor(
-                    out=r_sum[g][:, t, cols], in0=r_banks[g][t][:, cols], in1=d_sb[g][:, t, cols], op=ADD
+                    out=rhs_sum[g][:, s, lo:hi], in0=rhs_banks[g][s][:, lo:hi], in1=d_sb[g][:, s, lo:hi], op=ADD
                 )
 
-        def rhs_interleave(g, lo, hi):
-            interleave(r_grouped[g][:], r_sum[g][:], False, lo, hi, "scalar")
+        def rhs_interleave(copy, g, h):
+            strips = slice(h * STRIPS // 2, (h + 1) * STRIPS // 2)
+            interleave(copy, rhs_grouped[g][:], rhs_sum[g][:], strips, False)
 
-        def rhs_quantize(g, cols):
-            quantize(r_codes[g][:, cols], r_scales[g][:, cols], r_grouped[g][:, PACK * cols.start : PACK * cols.stop])
+        def rhs_quantize(g, h):
+            columns = slice(h * HALF, (h + 1) * HALF)
+            grouped = rhs_grouped[g][:, SLOTS * h * HALF : SLOTS * (h + 1) * HALF]
+            quantize(rhs_codes[g][:, columns], rhs_scales[g][:, columns], grouped)
 
-        grouped = {}
-        last = len(chunks) - 1
-        for n in range(len(chunks)):
-            which = chunks[n][0]
-            share = SHARE_FIRST if n == 0 else SHARE_H if n <= 8 else SHARE_LATE
-            if n >= 2 and chunks[n - 2][0] == "a":
-                rhs_pass(n - 2)
-            if 1 <= n <= 8:
-                h_matmul(2 * n - 2)
-                h_matmul(2 * n - 1)
-            if 2 <= n <= 9:
-                h_copy(2 * n - 4)
-                h_copy(2 * n - 3)
-            grouped[n] = stage.tile([P, KP * PACK], BF16, name="grouped", tag="grouped", bufs=3, align_bytes=64)
-            interleave(grouped[n][:], raw[n][:], which == "a", RUNS - share, RUNS, "scalar")
-            if n == 10:
-                rhs_interleave(0, 0, RUNS)
-            interleave(grouped[n][:], raw[n][:], which == "a", 0, RUNS - share, "vector")
-            if n >= 1:
-                quantize(codes[n - 1][:], scales[n - 1][:], grouped[n - 1][:])
-            if n == 0:
-                order_e_plane()
-                order_e_words(0)
-            if n == 2:
-                order_e_words(1)
-            if n in (4, 6, 8, 10):
-                h_quantize((n - 4) // 2)
-            if n == 9:
-                rhs_add(0, slice(0, T))
-        rhs_pass(last - 1)
-        quantize(codes[last][:], scales[last][:], grouped[last][:])
-        rhs_pass(last)
-        rhs_quantize(0, slice(0, T))
-
-        halves = [slice(h * HALF, (h + 1) * HALF) for h in range(2)]
-        for h in range(2):
-            rhs_add(1, halves[h])
-            rhs_interleave(1, h * RUNS // 2, (h + 1) * RUNS // 2)
-
+        x_bank_order = [0, 1, 4, 5, 6, 7, 2, 3]
         x_banks = {}
 
         def x_matmul(h, pair):
-            acc = bank(4 * (1 - h) + pair, [P, 2, HALF])
+            acc = bank(x_bank_order[4 * h + pair], [P, 2, HALF])
             x_banks[h, pair] = acc
-            for jj in range(2):
-                cols = slice(P * (2 * pair + jj), P * (2 * pair + jj + 1))
+            targets = slice(h * HALF, (h + 1) * HALF)
+            for j in range(2):
+                rows = slice(P * (2 * pair + j), P * (2 * pair + j + 1))
                 for g in range(GROUPS):
                     nc.tensor.matmul_mx(
-                        out=acc[:, jj, :],
-                        lhsT=h_codes[g][:, cols].bitcast(FP8X4),
-                        lhsT_scale=h_scales[g][:, cols],
-                        rhs=r_codes[g][:, halves[h]].bitcast(FP8X4),
-                        rhs_scale=r_scales[g][:, halves[h]],
+                        out=acc[:, j, :],
+                        lhsT=h_codes[g][:, rows].bitcast(FP8X4),
+                        lhsT_scale=h_scales[g][:, rows],
+                        rhs=rhs_codes[g][:, targets].bitcast(FP8X4),
+                        rhs_scale=rhs_scales[g][:, targets],
                         start=(g == 0),
                         stop=(g == GROUPS - 1),
                     )
 
         def x_finish(h, pair):
-            rows = slice(2 * pair, 2 * pair + 2)
-            total = stage.tile([P, 2, HALF], F32, name="total", tag="total", bufs=4)
-            nc.vector.tensor_tensor(out=total[:], in0=x_banks[h, pair][:], in1=c_sb[h][:, rows, :], op=ADD)
+            q, j = divmod(2 * pair, SLOTS)
+            targets = slice(h * HALF, (h + 1) * HALF)
+            total = stage.tile([P, 2, HALF], F32, name="total", tag="total")
+            nc.vector.tensor_tensor(out=total[:], in0=x_banks[h, pair][:], in1=c_sb[q][:, j : j + 2, targets], op=ADD)
             result = stage.tile([P, 2, HALF], F32, name="result", tag="result", bufs=8)
-            nc.scalar.activation(out=result[:], in_=total[:], func=RELU)
-            nc.sync.dma_start(out=out_rows[:, rows, halves[h]], in_=result[:])
+            nc.scalar.activation(out=result[:], in_=total[:], func=ACT.Relu)
+            nc.sync.dma_start(out=out_rows[:, q, j : j + 2, targets], in_=result[:])
 
-        rhs_quantize(1, halves[0])
-        for pair in range(4):
-            x_matmul(0, pair)
-        x_finish(0, 0)
-        rhs_quantize(1, halves[1])
+
+        group_0_done = first_a + SAMPLE_PASSES + 1
+        h_steps = H_EARLY // H_PER_STEP
+        h_issued = 0
+        for n in range(len(chunks)):
+            if n <= h_steps:
+                share = SHARE_BESIDE_H
+            elif n in (group_0_done, group_0_done + 1):
+                share = SHARE_BESIDE_ADDS
+            else:
+                share = SHARE_EVEN
+            is_a = n >= first_a
+
+            if n - 2 >= first_a:
+                rhs_pass(n - 2)
+            h_wanted = min(H_PER_STEP * n + H_LEAD, H_EARLY) if n >= 1 else 0
+            if n > group_0_done:
+                h_wanted = H_EARLY + 2
+            for unit in range(h_issued, h_wanted):
+                h_matmul(unit)
+            h_issued = h_wanted
+
+            chunk_grouped[n] = stage.tile([P, PASS * SLOTS], BF16, name="grouped", tag="grouped", align_bytes=64)
+            scalar_copy = copy_by_activation if n == 0 else nc.scalar.copy
+            interleave(scalar_copy, chunk_grouped[n][:], raw[n][:], slice(STRIPS - share, STRIPS), is_a)
+            if 1 <= n <= h_steps:
+                for unit in range(H_PER_STEP * (n - 1), H_PER_STEP * n):
+                    h_copy(unit)
+
+            interleave(nc.vector.tensor_copy, chunk_grouped[n][:], raw[n][:], slice(0, STRIPS - share), is_a)
+            if n > LOAD_BOUND_STEPS:
+                quantize_chunk(n - 1)
+            if n == 0:
+                order_e_scales()
+            if n < GROUPS:
+                order_e_codes(n)
+            if n < LOAD_BOUND_STEPS:
+                quantize_chunk(n)
+            copied_before = H_PER_STEP * (n - 1)
+            if 0 < copied_before <= H_EARLY and copied_before % 4 == 0:
+                h_quantize(copied_before // 4 - 1)
+            if n == group_0_done:
+                rhs_add(0, 0, T)
+
+
+        rhs_pass(last - 1)
+        rhs_interleave(nc.scalar.copy, 0, 0)
+        quantize_chunk(last)
+        rhs_pass(last)
+        for unit in (H_EARLY, H_EARLY + 1):
+            h_copy(unit)
+            h_matmul(unit + 2)
+        rhs_quantize(0, 0)
+        rhs_add(1, 0, HALF)
+        rhs_interleave(nc.vector.tensor_copy, 1, 0)
+        rhs_interleave(nc.scalar.copy, 0, 1)
+        h_copy(H_EARLY + 2)
+        h_copy(H_EARLY + 3)
+        rhs_add(1, HALF, HALF + QUARTER)
+        rhs_quantize(1, 0)
+        x_matmul(0, 0)
+        x_matmul(0, 1)
+        rhs_add(1, HALF + QUARTER, T)
+        rhs_interleave(nc.scalar.copy, 1, 1)
+        h_quantize(len(h_sets) - 1)
+        x_matmul(0, 2)
+        x_matmul(0, 3)
+        for g in range(GROUPS):
+            x_finish(0, g)
+            rhs_quantize(g, 1)
         for pair in range(4):
             x_matmul(1, pair)
-        for pair in range(1, 4):
-            x_finish(0, pair)
+        x_finish(0, 2)
+        x_finish(0, 3)
         for pair in range(4):
             x_finish(1, pair)

@@ -26,7 +26,7 @@ GROUPS = F // PASS
 HALF = T // 2
 QUARTER = T // 4
 
-SHARE_BESIDE_H, SHARE_EVEN, SHARE_BESIDE_ADDS = 12, 16, 24
+SHARE_FIRST, SHARE_BESIDE_H, SHARE_FREE, SHARE_LAST = 12, 8, 20, 16
 H_EARLY = 12
 H_PER_STEP = 2
 H_LEAD = 2
@@ -51,15 +51,22 @@ def tile_admm_nonnegative_lasso_step_s12_kernel(
             tile = psum.tile(shape, F32, name="bank%d" % number, tag="bank%d" % number)
             return tile
 
+        shared_pass = SAMPLE_PASSES - 1
         chunks = [(b, 0, k) for k in range(SAMPLE_PASSES)]
-        chunks.extend((a, g, k) for g in range(GROUPS) for k in range(SAMPLE_PASSES))
+        chunks.extend((a, 0, k) for k in range(SAMPLE_PASSES))
+        chunks.extend((a, 1, (shared_pass + k) % SAMPLE_PASSES) for k in range(SAMPLE_PASSES))
         first_a = SAMPLE_PASSES
+        shared = first_a + shared_pass
         last = len(chunks) - 1
-        raw = [held("raw%d" % n, [P, SLOTS, PASS], BF16) for n in range(len(chunks))]
+        shared_rows = held("shared_rows", [P, SLOTS, F], BF16)
+        raw = {shared + g: shared_rows[:, :, g * PASS : (g + 1) * PASS] for g in range(GROUPS)}
+        for n in range(len(chunks)):
+            if n not in raw:
+                raw[n] = held("raw%d" % n, [P, SLOTS, PASS], BF16)[:]
         codes = [held("codes%d" % n, [P, PASS], U32) for n in range(len(chunks))]
         scales = [held("scales%d" % n, [P, PASS], U8) for n in range(len(chunks))]
         l_codes = [held("l_codes%d" % q, [P, FACTOR_PASSES, 2 * PASS], U8) for q in range(GROUPS)]
-        e_loaded = [held("e_loaded%d" % g, [P, FACTOR_PASSES, 2 * PASS], U8) for g in range(GROUPS)]
+        e_loaded = held("e_loaded", [P, FACTOR_PASSES, 2 * F], U8)
         e_codes = [held("e_codes%d" % g, [P, FACTOR_PASSES, 2 * PASS], U8) for g in range(GROUPS)]
         l_scale_tile = held("l_scale_tile", [P, FACTOR_PASSES, F], U8)
         e_scale_loaded = held("e_scale_loaded", [P, FACTOR_PASSES, F], U8)
@@ -68,7 +75,8 @@ def tile_admm_nonnegative_lasso_step_s12_kernel(
         c_sb = [held("c_sb%d" % q, [P, SLOTS, T], BF16) for q in range(GROUPS)]
         h_codes = [held("h_codes%d" % g, [P, F], U32) for g in range(GROUPS)]
         h_scales = [held("h_scales%d" % g, [P, F], U8) for g in range(GROUPS)]
-        rhs_sum = [held("rhs_sum%d" % g, [P, SLOTS, T], BF16) for g in range(GROUPS)]
+        rhs_pieces = [(0, 0, HALF), (0, HALF, T), (1, 0, HALF), (1, HALF, HALF + QUARTER), (1, HALF + QUARTER, T)]
+        rhs_sum = [held("rhs_sum%d" % n, [P, SLOTS, hi - lo], BF16) for n, (g, lo, hi) in enumerate(rhs_pieces)]
         rhs_grouped = [held("rhs_grouped%d" % g, [P, T * SLOTS], BF16) for g in range(GROUPS)]
         rhs_codes = [held("rhs_codes%d" % g, [P, T], U32) for g in range(GROUPS)]
         rhs_scales = [held("rhs_scales%d" % g, [P, T], U8) for g in range(GROUPS)]
@@ -78,12 +86,14 @@ def tile_admm_nonnegative_lasso_step_s12_kernel(
 
         def load_chunk(n):
             source, g, k = chunks[n]
-            rows = source[k * PASS : (k + 1) * PASS, g * PASS : (g + 1) * PASS]
-            nc.sync.dma_start(out=raw[n][:], in_=rows.rearrange("(p s) w -> p s w", s=SLOTS))
+            rows = source[k * PASS : (k + 1) * PASS, :].rearrange("(p s) w -> p s w", s=SLOTS)
+            if n == shared:
+                nc.sync.dma_start(out=shared_rows[:], in_=rows)
+            elif n != shared + 1:
+                nc.sync.dma_start(out=raw[n], in_=rows[:, :, g * PASS : (g + 1) * PASS])
 
-        def load_codes(tile, words, g):
-            columns = words[:, :, 2 * PASS * g : 2 * PASS * (g + 1)].rearrange("k p n -> p k n")
-            nc.sync.dma_start(out=tile[:].bitcast(I32), in_=columns.bitcast(I32))
+        def load_codes(tile, words):
+            nc.sync.dma_start(out=tile[:].bitcast(I32), in_=words.rearrange("k p n -> p k n").bitcast(I32))
 
         def load_scales(tile, rows):
             by_r = rows.rearrange("k (q r) n -> r q k n", r=4)
@@ -99,14 +109,13 @@ def tile_admm_nonnegative_lasso_step_s12_kernel(
         nc.vector.memset(l_scale_tile[:].bitcast(I32), 0)
 
         load_chunk(0)
-        load_codes(e_loaded[0], e_words, 0)
+        load_codes(e_loaded, e_words)
         load_scales(e_scale_loaded, e_scales)
-        load_codes(l_codes[0], l_words, 0)
+        load_codes(l_codes[0], l_words[:, :, : 2 * PASS])
         load_scales(l_scale_tile, l_scales)
         load_chunk(1)
-        load_codes(e_loaded[1], e_words, 1)
         load_chunk(2)
-        load_codes(l_codes[1], l_words, 1)
+        load_codes(l_codes[1], l_words[:, :, 2 * PASS :])
         for n in range(3, last - 1):
             load_chunk(n)
         load_d(0)
@@ -126,7 +135,7 @@ def tile_admm_nonnegative_lasso_step_s12_kernel(
         def order_e_codes(g):
             nc.vector.tensor_copy(
                 out=e_codes[g][:].bitcast(I32).rearrange("p k (s u w) -> p k s u w", s=SLOTS, w=2),
-                in_=e_loaded[g][:].bitcast(I32).rearrange("p k (u s w) -> p k s u w", s=SLOTS, w=2),
+                in_=e_loaded[:].bitcast(I32).rearrange("p k (g u s w) -> p g k s u w", g=GROUPS, s=SLOTS, w=2)[:, g],
             )
 
         def interleave(copy, grouped, rows, strips, stationary):
@@ -184,7 +193,8 @@ def tile_admm_nonnegative_lasso_step_s12_kernel(
 
         def rhs_pass(n):
             source, g, k = chunks[n]
-            if k == 0:
+            place = n % SAMPLE_PASSES
+            if place == 0:
                 rhs_banks[g] = [bank(SLOTS * g + s, [P, T]) for s in range(SLOTS)]
             for s in range(SLOTS):
                 columns = slice(P * s, P * (s + 1))
@@ -194,19 +204,20 @@ def tile_admm_nonnegative_lasso_step_s12_kernel(
                     lhsT_scale=scales[n][:, columns],
                     rhs=codes[k][:].bitcast(FP8X4),
                     rhs_scale=scales[k][:],
-                    start=(k == 0),
-                    stop=(k == SAMPLE_PASSES - 1),
+                    start=(place == 0),
+                    stop=(place == SAMPLE_PASSES - 1),
                 )
 
-        def rhs_add(g, lo, hi):
-            for s in range(SLOTS):
+        def rhs_add(piece, slots):
+            g, lo, hi = rhs_pieces[piece]
+            for s in slots:
                 nc.vector.tensor_tensor(
-                    out=rhs_sum[g][:, s, lo:hi], in0=rhs_banks[g][s][:, lo:hi], in1=d_sb[g][:, s, lo:hi], op=ADD
+                    out=rhs_sum[piece][:, s, :], in0=rhs_banks[g][s][:, lo:hi], in1=d_sb[g][:, s, lo:hi], op=ADD
                 )
 
-        def rhs_interleave(copy, g, h):
-            strips = slice(h * STRIPS // 2, (h + 1) * STRIPS // 2)
-            interleave(copy, rhs_grouped[g][:], rhs_sum[g][:], strips, False)
+        def rhs_interleave(copy, piece):
+            g, lo, hi = rhs_pieces[piece]
+            interleave(copy, rhs_grouped[g][:, SLOTS * lo : SLOTS * hi], rhs_sum[piece][:], slice(None), False)
 
         def rhs_quantize(g, h):
             columns = slice(h * HALF, (h + 1) * HALF)
@@ -247,12 +258,14 @@ def tile_admm_nonnegative_lasso_step_s12_kernel(
         h_steps = H_EARLY // H_PER_STEP
         h_issued = 0
         for n in range(len(chunks)):
-            if n <= h_steps:
+            if n == 0:
+                share = SHARE_FIRST
+            elif n <= h_steps:
                 share = SHARE_BESIDE_H
-            elif n in (group_0_done, group_0_done + 1):
-                share = SHARE_BESIDE_ADDS
+            elif n < last:
+                share = SHARE_FREE
             else:
-                share = SHARE_EVEN
+                share = SHARE_LAST
             is_a = n >= first_a
 
             if n - 2 >= first_a:
@@ -266,12 +279,12 @@ def tile_admm_nonnegative_lasso_step_s12_kernel(
 
             chunk_grouped[n] = stage.tile([P, PASS * SLOTS], BF16, name="grouped", tag="grouped", align_bytes=64)
             scalar_copy = copy_by_activation if n == 0 else nc.scalar.copy
-            interleave(scalar_copy, chunk_grouped[n][:], raw[n][:], slice(STRIPS - share, STRIPS), is_a)
+            interleave(scalar_copy, chunk_grouped[n][:], raw[n], slice(STRIPS - share, STRIPS), is_a)
             if 1 <= n <= h_steps:
                 for unit in range(H_PER_STEP * (n - 1), H_PER_STEP * n):
                     h_copy(unit)
 
-            interleave(nc.vector.tensor_copy, chunk_grouped[n][:], raw[n][:], slice(0, STRIPS - share), is_a)
+            interleave(nc.vector.tensor_copy, chunk_grouped[n][:], raw[n], slice(0, STRIPS - share), is_a)
             if n > LOAD_BOUND_STEPS:
                 quantize_chunk(n - 1)
             if n == 0:
@@ -284,34 +297,38 @@ def tile_admm_nonnegative_lasso_step_s12_kernel(
             if 0 < copied_before <= H_EARLY and copied_before % 4 == 0:
                 h_quantize(copied_before // 4 - 1)
             if n == group_0_done:
-                rhs_add(0, 0, T)
+                rhs_add(0, (2, 3))
+                rhs_add(1, (2, 3))
 
 
         rhs_pass(last - 1)
-        rhs_interleave(nc.scalar.copy, 0, 0)
         quantize_chunk(last)
         rhs_pass(last)
         for unit in (H_EARLY, H_EARLY + 1):
             h_copy(unit)
             h_matmul(unit + 2)
+        for piece in (0, 1):
+            rhs_add(piece, (0, 1))
+            rhs_interleave(nc.scalar.copy, piece)
+        rhs_add(2, range(SLOTS))
         rhs_quantize(0, 0)
-        rhs_add(1, 0, HALF)
-        rhs_interleave(nc.vector.tensor_copy, 1, 0)
-        rhs_interleave(nc.scalar.copy, 0, 1)
+        rhs_interleave(nc.vector.tensor_copy, 2)
         h_copy(H_EARLY + 2)
         h_copy(H_EARLY + 3)
-        rhs_add(1, HALF, HALF + QUARTER)
+        rhs_add(3, range(SLOTS))
+        rhs_interleave(nc.scalar.copy, 3)
         rhs_quantize(1, 0)
         x_matmul(0, 0)
         x_matmul(0, 1)
-        rhs_add(1, HALF + QUARTER, T)
-        rhs_interleave(nc.scalar.copy, 1, 1)
+        rhs_add(4, range(SLOTS))
+        rhs_interleave(nc.scalar.copy, 4)
         h_quantize(len(h_sets) - 1)
         x_matmul(0, 2)
         x_matmul(0, 3)
-        for g in range(GROUPS):
-            x_finish(0, g)
-            rhs_quantize(g, 1)
+        x_finish(0, 0)
+        rhs_quantize(0, 1)
+        x_finish(0, 1)
+        rhs_quantize(1, 1)
         for pair in range(4):
             x_matmul(1, pair)
         x_finish(0, 2)

from contextlib import ExitStack

import concourse.mybir as mybir

M, F, D, T = 2048, 1024, 1024, 512
FLOPS = 2 * D * F * F + 2 * M * F * T + 2 * F * F * T

F32 = mybir.dt.float32
BF16 = mybir.dt.bfloat16
I32 = mybir.dt.int32
U32 = mybir.dt.uint32
U8 = mybir.dt.uint8
FP8X4 = mybir.dt.float8_e4m3fn_x4
FP4X4 = mybir.dt.float4_e2m1fn_x4
ADD = mybir.AluOpType.add
ACT = mybir.ActivationFunctionType

P = 128
SLOTS = 4
PASS = P * SLOTS
RUN = 4
STRIPS = PASS // (RUN * SLOTS)
SAMPLE_PASSES = M // PASS
FACTOR_PASSES = D // PASS
GROUPS = F // PASS
HALF = T // 2
QUARTER = T // 4

SHARE_FIRST, SHARE_BESIDE_H, SHARE_FREE, SHARE_LAST = 12, 8, 20, 16
H_EARLY = 12
H_PER_STEP = 2
H_LEAD = 2
LOAD_BOUND_STEPS = 3


def tile_admm_nonnegative_lasso_step_s12_kernel(
    tc, l_words, l_scales, e_words, e_scales, a, b, d, c, out
):
    nc = tc.nc
    with ExitStack() as ctx:
        keep = ctx.enter_context(tc.tile_pool(name="keep", bufs=1))
        stage = ctx.enter_context(tc.tile_pool(name="stage", bufs=4))
        psum = ctx.enter_context(tc.psum_pool(name="psum", bufs=1))
        ctx.enter_context(tc.manual_schedule())

        def held(name, shape, dtype):
            tile = keep.tile(shape, dtype, name=name, tag=name, align_bytes=64)
            return tile

        def bank(number, shape):
            tile = psum.tile(shape, F32, name="bank%d" % number, tag="bank%d" % number)
            return tile

        shared_pass = SAMPLE_PASSES - 1
        chunks = [(b, 0, k) for k in range(SAMPLE_PASSES)]
        chunks.extend((a, 0, k) for k in range(SAMPLE_PASSES))
        chunks.extend((a, 1, (shared_pass + k) % SAMPLE_PASSES) for k in range(SAMPLE_PASSES))
        first_a = SAMPLE_PASSES
        shared = first_a + shared_pass
        last = len(chunks) - 1
        shared_rows = held("shared_rows", [P, SLOTS, F], BF16)
        raw = {shared + g: shared_rows[:, :, g * PASS : (g + 1) * PASS] for g in range(GROUPS)}
        for n in range(len(chunks)):
            if n not in raw:
                raw[n] = held("raw%d" % n, [P, SLOTS, PASS], BF16)[:]
        codes = [held("codes%d" % n, [P, PASS], U32) for n in range(len(chunks))]
        scales = [held("scales%d" % n, [P, PASS], U8) for n in range(len(chunks))]
        l_codes = [held("l_codes%d" % q, [P, FACTOR_PASSES, 2 * PASS], U8) for q in range(GROUPS)]
        e_loaded = held("e_loaded", [P, FACTOR_PASSES, 2 * F], U8)
        e_codes = [held("e_codes%d" % g, [P, FACTOR_PASSES, 2 * PASS], U8) for g in range(GROUPS)]
        l_scale_tile = held("l_scale_tile", [P, FACTOR_PASSES, F], U8)
        e_scale_loaded = held("e_scale_loaded", [P, FACTOR_PASSES, F], U8)
        e_scale_tile = held("e_scale_tile", [P, FACTOR_PASSES, F], U8)
        d_sb = [held("d_sb%d" % g, [P, SLOTS, T], BF16) for g in range(GROUPS)]
        c_sb = [held("c_sb%d" % q, [P, SLOTS, T], BF16) for q in range(GROUPS)]
        h_codes = [held("h_codes%d" % g, [P, F], U32) for g in range(GROUPS)]
        h_scales = [held("h_scales%d" % g, [P, F], U8) for g in range(GROUPS)]
        rhs_pieces = [(0, 0, HALF), (0, HALF, T), (1, 0, HALF), (1, HALF, HALF + QUARTER), (1, HALF + QUARTER, T)]
        rhs_sum = [held("rhs_sum%d" % n, [P, SLOTS, hi - lo], BF16) for n, (g, lo, hi) in enumerate(rhs_pieces)]
        rhs_grouped = [held("rhs_grouped%d" % g, [P, T * SLOTS], BF16) for g in range(GROUPS)]
        rhs_codes = [held("rhs_codes%d" % g, [P, T], U32) for g in range(GROUPS)]
        rhs_scales = [held("rhs_scales%d" % g, [P, T], U8) for g in range(GROUPS)]
        c_rows = c.rearrange("(q p j) n -> p q j n", p=P, j=SLOTS)
        out_rows = out.rearrange("(q p j) n -> p q j n", p=P, j=SLOTS)


        def load_chunk(n):
            source, g, k = chunks[n]
            rows = source[k * PASS : (k + 1) * PASS, :].rearrange("(p s) w -> p s w", s=SLOTS)
            if n == shared:
                nc.sync.dma_start(out=shared_rows[:], in_=rows)
            elif n != shared + 1:
                nc.sync.dma_start(out=raw[n], in_=rows[:, :, g * PASS : (g + 1) * PASS])

        def load_codes(tile, words):
            nc.sync.dma_start(out=tile[:].bitcast(I32), in_=words.rearrange("k p n -> p k n").bitcast(I32))

        def load_scales(tile, rows):
            by_r = rows.rearrange("k (q r) n -> r q k n", r=4)
            for r in range(4):
                nc.sync.dma_start(out=tile[r:P:32, :, :].bitcast(I32), in_=by_r[r].bitcast(I32))

        def load_d(g):
            by_i = d[g * PASS : (g + 1) * PASS, :].rearrange("(u s i) n -> i u s n", s=SLOTS, i=RUN)
            for i in range(RUN):
                nc.sync.dma_start(out=d_sb[g][i:P:RUN, :, :], in_=by_i[i])

        nc.vector.memset(e_scale_loaded[:].bitcast(I32), 0)
        nc.vector.memset(l_scale_tile[:].bitcast(I32), 0)

        load_chunk(0)
        load_codes(e_loaded, e_words)
        load_scales(e_scale_loaded, e_scales)
        load_codes(l_codes[0], l_words[:, :, : 2 * PASS])
        load_scales(l_scale_tile, l_scales)
        load_chunk(1)
        load_chunk(2)
        load_codes(l_codes[1], l_words[:, :, 2 * PASS :])
        for n in range(3, last - 1):
            load_chunk(n)
        load_d(0)
        load_chunk(last - 1)
        load_chunk(last)
        load_d(1)
        for q in range(GROUPS):
            nc.sync.dma_start(out=c_sb[q][:], in_=c_rows[:, q, :, :])


        def order_e_scales():
            nc.vector.tensor_copy(
                out=e_scale_tile[:].bitcast(I32).rearrange("p k (g s u) -> p k g s u", g=GROUPS, s=SLOTS),
                in_=e_scale_loaded[:].bitcast(I32).rearrange("p k (g u s) -> p k g s u", g=GROUPS, s=SLOTS),
            )

        def order_e_codes(g):
            nc.vector.tensor_copy(
                out=e_codes[g][:].bitcast(I32).rearrange("p k (s u w) -> p k s u w", s=SLOTS, w=2),
                in_=e_loaded[:].bitcast(I32).rearrange("p k (g u s w) -> p g k s u w", g=GROUPS, s=SLOTS, w=2)[:, g],
            )

        def interleave(copy, grouped, rows, strips, stationary):
            order = "p (t u i s) -> p u t i s" if stationary else "p (u t i s) -> p u t i s"
            copy(
                out=grouped.rearrange(order, t=SLOTS, i=RUN, s=SLOTS)[:, strips],
                in_=rows.rearrange("p s (u t i) -> p u t i s", t=SLOTS, i=RUN)[:, strips],
            )

        def copy_by_activation(out, in_):
            nc.scalar.activation(out=out, in_=in_, func=ACT.Copy)

        def quantize(code_ap, scale_ap, grouped):
            nc.vector.quantize_mx(out=code_ap.bitcast(FP8X4), scales=scale_ap, in_=grouped)

        chunk_grouped = {}

        def quantize_chunk(n):
            quantize(codes[n][:], scales[n][:], chunk_grouped[n][:])

        h_sets = [(g, q) for q in range(GROUPS) for g in range(GROUPS)]
        h_banks = {}
        h_grouped = {}

        def h_matmul(unit):
            g, q = h_sets[unit // 4]
            moving = unit % 4
            acc = bank((4 + unit) % 8 if unit < H_EARLY else 2 + unit % 2, [P, SLOTS, P])
            h_banks[unit] = acc
            for s in range(SLOTS):
                for k in range(FACTOR_PASSES):
                    nc.tensor.matmul_mx(
                        out=acc[:, s, :],
                        lhsT=e_codes[g][:, k, 2 * P * s : 2 * P * (s + 1)].bitcast(FP4X4),
                        lhsT_scale=e_scale_tile[:, k, g * PASS + P * s : g * PASS + P * (s + 1)],
                        rhs=l_codes[q][:, k, 2 * P * moving : 2 * P * (moving + 1)].bitcast(FP4X4),
                        rhs_scale=l_scale_tile[:, k, q * PASS + P * moving : q * PASS + P * (moving + 1)],
                        start=(k == 0),
                        stop=(k == FACTOR_PASSES - 1),
                    )

        def h_copy(unit):
            n, w = divmod(unit, 4)
            if w == 0:
                h_grouped[n] = stage.tile([P, PASS * SLOTS], BF16, name="h_grouped", tag="h_grouped", align_bytes=64)
            target = h_grouped[n][:].rearrange("p (j w m s) -> p w j m s", j=SLOTS, w=4, s=SLOTS)[:, w]
            nc.scalar.copy(out=target, in_=h_banks[unit][:].rearrange("p s (m j) -> p j m s", j=SLOTS))

        def h_quantize(n):
            g, q = h_sets[n]
            columns = slice(q * PASS, (q + 1) * PASS)
            quantize(h_codes[g][:, columns], h_scales[g][:, columns], h_grouped[n][:])

        rhs_banks = {}

        def rhs_pass(n):
            source, g, k = chunks[n]
            place = n % SAMPLE_PASSES
            if place == 0:
                rhs_banks[g] = [bank(SLOTS * g + s, [P, T]) for s in range(SLOTS)]
            for s in range(SLOTS):
                columns = slice(P * s, P * (s + 1))
                nc.tensor.matmul_mx(
                    out=rhs_banks[g][s][:],
                    lhsT=codes[n][:, columns].bitcast(FP8X4),
                    lhsT_scale=scales[n][:, columns],
                    rhs=codes[k][:].bitcast(FP8X4),
                    rhs_scale=scales[k][:],
                    start=(place == 0),
                    stop=(place == SAMPLE_PASSES - 1),
                )

        def rhs_add(piece, slots):
            g, lo, hi = rhs_pieces[piece]
            for s in slots:
                nc.vector.tensor_tensor(
                    out=rhs_sum[piece][:, s, :], in0=rhs_banks[g][s][:, lo:hi], in1=d_sb[g][:, s, lo:hi], op=ADD
                )

        def rhs_interleave(copy, piece):
            g, lo, hi = rhs_pieces[piece]
            interleave(copy, rhs_grouped[g][:, SLOTS * lo : SLOTS * hi], rhs_sum[piece][:], slice(None), False)

        def rhs_quantize(g, h):
            columns = slice(h * HALF, (h + 1) * HALF)
            grouped = rhs_grouped[g][:, SLOTS * h * HALF : SLOTS * (h + 1) * HALF]
            quantize(rhs_codes[g][:, columns], rhs_scales[g][:, columns], grouped)

        x_bank_order = [0, 1, 4, 5, 6, 7, 2, 3]
        x_banks = {}

        def x_matmul(h, pair):
            acc = bank(x_bank_order[4 * h + pair], [P, 2, HALF])
            x_banks[h, pair] = acc
            targets = slice(h * HALF, (h + 1) * HALF)
            for j in range(2):
                rows = slice(P * (2 * pair + j), P * (2 * pair + j + 1))
                for g in range(GROUPS):
                    nc.tensor.matmul_mx(
                        out=acc[:, j, :],
                        lhsT=h_codes[g][:, rows].bitcast(FP8X4),
                        lhsT_scale=h_scales[g][:, rows],
                        rhs=rhs_codes[g][:, targets].bitcast(FP8X4),
                        rhs_scale=rhs_scales[g][:, targets],
                        start=(g == 0),
                        stop=(g == GROUPS - 1),
                    )

        def x_finish(h, pair):
            q, j = divmod(2 * pair, SLOTS)
            targets = slice(h * HALF, (h + 1) * HALF)
            total = stage.tile([P, 2, HALF], F32, name="total", tag="total")
            nc.vector.tensor_tensor(out=total[:], in0=x_banks[h, pair][:], in1=c_sb[q][:, j : j + 2, targets], op=ADD)
            result = stage.tile([P, 2, HALF], F32, name="result", tag="result", bufs=8)
            nc.scalar.activation(out=result[:], in_=total[:], func=ACT.Relu)
            nc.sync.dma_start(out=out_rows[:, q, j : j + 2, targets], in_=result[:])


        group_0_done = first_a + SAMPLE_PASSES + 1
        h_steps = H_EARLY // H_PER_STEP
        h_issued = 0
        for n in range(len(chunks)):
            if n == 0:
                share = SHARE_FIRST
            elif n <= h_steps:
                share = SHARE_BESIDE_H
            elif n < last:
                share = SHARE_FREE
            else:
                share = SHARE_LAST
            is_a = n >= first_a

            if n - 2 >= first_a:
                rhs_pass(n - 2)
            h_wanted = min(H_PER_STEP * n + H_LEAD, H_EARLY) if n >= 1 else 0
            if n > group_0_done:
                h_wanted = H_EARLY + 2
            for unit in range(h_issued, h_wanted):
                h_matmul(unit)
            h_issued = h_wanted

            chunk_grouped[n] = stage.tile([P, PASS * SLOTS], BF16, name="grouped", tag="grouped", align_bytes=64)
            scalar_copy = copy_by_activation if n == 0 else nc.scalar.copy
            interleave(scalar_copy, chunk_grouped[n][:], raw[n], slice(STRIPS - share, STRIPS), is_a)
            if 1 <= n <= h_steps:
                for unit in range(H_PER_STEP * (n - 1), H_PER_STEP * n):
                    h_copy(unit)

            interleave(nc.vector.tensor_copy, chunk_grouped[n][:], raw[n], slice(0, STRIPS - share), is_a)
            if n > LOAD_BOUND_STEPS:
                quantize_chunk(n - 1)
            if n == 0:
                order_e_scales()
            if n < GROUPS:
                order_e_codes(n)
            if n < LOAD_BOUND_STEPS:
                quantize_chunk(n)
            copied_before = H_PER_STEP * (n - 1)
            if 0 < copied_before <= H_EARLY and copied_before % 4 == 0:
                h_quantize(copied_before // 4 - 1)
            if n == group_0_done:
                rhs_add(0, (2, 3))
                rhs_add(1, (2, 3))


        rhs_pass(last - 1)
        quantize_chunk(last)
        rhs_pass(last)
        for unit in (H_EARLY, H_EARLY + 1):
            h_copy(unit)
            h_matmul(unit + 2)
        for piece in (0, 1):
            rhs_add(piece, (0, 1))
            rhs_interleave(nc.scalar.copy, piece)
        rhs_add(2, range(SLOTS))
        rhs_quantize(0, 0)
        rhs_interleave(nc.vector.tensor_copy, 2)
        h_copy(H_EARLY + 2)
        h_copy(H_EARLY + 3)
        rhs_add(3, range(SLOTS))
        rhs_interleave(nc.scalar.copy, 3)
        rhs_quantize(1, 0)
        x_matmul(0, 0)
        x_matmul(0, 1)
        rhs_add(4, range(SLOTS))
        rhs_interleave(nc.scalar.copy, 4)
        h_quantize(len(h_sets) - 1)
        x_matmul(0, 2)
        x_matmul(0, 3)
        x_finish(0, 0)
        rhs_quantize(0, 1)
        x_finish(0, 1)
        rhs_quantize(1, 1)
        for pair in range(4):
            x_matmul(1, pair)
        x_finish(0, 2)
        x_finish(0, 3)
        for pair in range(4):
            x_finish(1, pair)
